import numpy as np
import ml_dtypes


def mxq(x, axis, fmt="e4m3"):
    dtype, down = {"e4m3": (ml_dtypes.float8_e4m3fn, 7), "e5m2": (ml_dtypes.float8_e5m2, 14)}[fmt]
    v = np.moveaxis(np.asarray(x, np.float32).astype(ml_dtypes.bfloat16).astype(np.float64), axis, -1)
    blocks = v.reshape(v.shape[:-1] + (-1, 32))
    amax = np.abs(blocks).max(-1, keepdims=True)
    byte = np.maximum(np.where(amax > 0, np.frexp(amax)[1] - 1 + 127, 0) - down, 1)
    scale = np.exp2(byte - 127.0)
    codes = (blocks / scale).astype(np.float32).astype(dtype).astype(np.float64)
    return np.moveaxis((codes * scale).reshape(v.shape), -1, axis)


WIDE = False


def mx_kscale(k):
    if not WIDE:
        return np.ones(k)
    levels = np.array([10, -10, 5, -5, 0])
    if k % 512:
        return np.exp2(np.random.permutation(np.resize(levels, k // 32))).repeat(32)
    a = np.empty((k // 512, 16))
    for p in range(k // 512):
        a[p, :8] = np.random.permutation(np.resize(levels, 8))
        for g in range(8):
            far = levels[np.abs(levels - a[p, g]) >= 10]
            a[p, g + 8] = far[np.random.randint(len(far))]
    return np.exp2(a.ravel()).repeat(32)


def f64(x):
    return np.asarray(x).astype(np.float64)


def striped(idx):
    return np.tile(idx.reshape(-1, 16).T, (8, 1)).astype(np.uint16)


def unstriped(offs):
    return offs[:16].T.reshape(-1).astype(np.int64)


def striped8(idx):
    return np.concatenate([x.reshape(-1, 16).T for x in idx]).astype(np.uint16)


def runs(offs, k):
    lists = np.stack([offs[16 * r : 16 * r + 16].T.reshape(-1) for r in range(8)]).astype(np.int64)
    return lists[np.arange(k) % 512 // 64]


def pack_weight(w):
    k, n = w.shape
    w = f64(np.asarray(w, np.float32).astype(ml_dtypes.bfloat16)).reshape(k // 32, 32, n)
    amax = np.abs(w).max(1)
    byte = np.clip(np.where(amax > 0, np.frexp(amax)[1] - 1 + 127 - 7, 1), 1, 254)
    scaled = (w * np.exp2(127.0 - byte)[:, None, :]).reshape(k, n).astype(np.float32)
    words = np.ascontiguousarray(scaled.reshape(k // 512, 128, 4, n).transpose(0, 1, 3, 2)).astype(ml_dtypes.float8_e4m3fn).view(np.uint8)
    return words, np.ascontiguousarray(byte.astype(np.uint8).reshape(k // 512, 16, n))


def unpack_weight(words, scales):
    g, p, n, _ = words.shape
    vals = np.ascontiguousarray(words).view(ml_dtypes.float8_e4m3fn).astype(np.float64) * np.repeat(np.exp2(scales.astype(np.float64) - 127.0), 8, axis=1)[..., None]
    return vals.transpose(0, 1, 3, 2).reshape(g * 512, n)


def sigmoid(v):
    return 1.0 / (1.0 + np.exp(-np.maximum(v, -700.0)))


K, T, S, H = 512, 2048, 256, 512


def setup_inputs():
    n = np.random.standard_normal
    s = mx_kscale(K)[:, None]
    u = mx_kscale(H)
    packed_xT = pack_weight(n((K, T)) * s)
    return {
        "x_words": packed_xT[0],
        "x_scales": packed_xT[1],
        "w1": (n((K, H)) / np.sqrt(K) / s).astype(np.float32),
        "gn": (np.random.uniform(0.5, 1.5, (H, 1)) * u[:, None]).astype(np.float32),
        "w2": (n((H, H)) / np.sqrt(H) / u[:, None]).astype(np.float32),
        "tau": np.random.uniform(0.3, 0.9, (H, 1)).astype(np.float32),
        "offs": striped(np.random.permutation(T)[:S]),
        "n1": striped8(np.stack([np.random.permutation(S) for _ in range(8)])),
        "n2": striped8(np.stack([np.random.permutation(S) for _ in range(8)])),
        "n3": striped8(np.stack([np.random.permutation(S) for _ in range(8)])),
        "n4": striped(np.random.permutation(S)),
        "n5": striped(np.random.permutation(S)),
    }


def reference(x_words, x_scales, w1, gn, w2, tau, offs, n1, n2, n3, n4, n5):
    xq = unpack_weight(x_words, x_scales)[:, unstriped(offs)]
    y = mxq(f64(w1), 0, "e4m3").T @ xq
    st = y * (sigmoid(y[np.arange(H)[:, None], runs(n1, H)]))
    z = f64(gn) * (st - (st[np.arange(H)[:, None], runs(n2, H)]))
    w2q = mxq(f64(w2), 0, "e4m3")
    a = w2q.T @ mxq(z, 0, "e4m3")
    z2 = f64(gn) * (y - (y[np.arange(H)[:, None], runs(n3, H)]))
    b = w2q.T @ mxq(z2, 0, "e4m3")
    top = b.max(axis=1, keepdims=True)
    ea = np.exp(f64(tau) * (b[:, unstriped(n4)] - top))
    return (0.5 * (a - a[:, unstriped(n5)])) / (ea + 0.25)

@@ -1,0 +1,219 @@
+from contextlib import ExitStack
+
+import concourse.mybir as mybir
+
+K, T, S, H = 512, 2048, 256, 512
+FLOPS = 3 * 2 * 512 * 512 * 256
+
+F32 = mybir.dt.float32
+BF16 = mybir.dt.bfloat16
+I32 = mybir.dt.int32
+U32 = mybir.dt.uint32
+U16 = mybir.dt.uint16
+U8 = mybir.dt.uint8
+FP8X4 = mybir.dt.float8_e4m3fn_x4
+ALU = mybir.AluOpType
+ACT = mybir.ActivationFunctionType
+
+P = 128
+PACK = 4
+WIN = 2 * S
+
+
+def tile_picked_tieqxbhopgdif_none_p_kernel(
+    tc, x_words, x_scales, w1, gn, w2, tau, offs, n1, n2, n3, n4, n5, out
+):
+    nc = tc.nc
+    with ExitStack() as ctx:
+        lists = ctx.enter_context(tc.tile_pool(name="lists", bufs=1))
+        sb = ctx.enter_context(tc.tile_pool(name="sb", bufs=1))
+        ps = ctx.enter_context(tc.psum_pool(name="ps", bufs=1))
+
+        def list_tile(name):
+            return lists.tile([P, S // 16], U16, name=name)
+
+        offs_t, n1_t, n2_t, n3_t, n4_t, n5_t = [list_tile(n) for n in ("offs", "n1", "n2", "n3", "n4", "n5")]
+
+        xw = sb.tile([P, T], U32, name="xw")
+        xs = sb.tile([P, T], U8, name="xs")
+        xs_in = sb.tile([P, T], U8, name="xs_in")
+        w1_raw = [sb.tile([P, PACK, H // 2], F32, name="w1_raw%d" % h) for h in range(2)]
+        w2_raw = sb.tile([P, PACK, H], F32, name="w2_raw")
+        gn_t = sb.tile([P, PACK], F32, name="gn")
+        tau_t = sb.tile([P, PACK], F32, name="tau")
+
+        nc.vector.memset(xs[:].bitcast(I32), 0)
+        w1_rows = w1.rearrange("(p j) c -> p j c", j=PACK)
+
+        def load_scale_rows(queue, q):
+            queue.dma_start(
+                out=xs_in[32 * q : 32 * q + 4, :].bitcast(I32), in_=x_scales[0, 4 * q : 4 * q + 4, :].bitcast(I32)
+            )
+
+        nc.sync.dma_start(out=w1_raw[0][:], in_=w1_rows[:, :, :256])
+        for q in range(3):
+            load_scale_rows(nc.scalar, q)
+        load_scale_rows(nc.sync, 3)
+        nc.sync.dma_start(out=w1_raw[1][:], in_=w1_rows[:, :, 256:])
+        nc.sync.dma_start(offs_t[:], offs)
+        nc.sync.dma_start(out=xw[:].bitcast(I32), in_=x_words[0].rearrange("p c r -> p (c r)").bitcast(I32))
+        nc.sync.dma_start(out=gn_t[:], in_=gn.rearrange("(p t) o -> p (t o)", t=PACK))
+        nc.sync.dma_start(n3_t[:], n3)
+        nc.sync.dma_start(out=w2_raw[:], in_=w2.rearrange("(p j) c -> p j c", j=PACK))
+        nc.sync.dma_start(n1_t[:], n1)
+        nc.sync.dma_start(n2_t[:], n2)
+        nc.sync.dma_start(out=tau_t[:], in_=tau.rearrange("(p t) o -> p (t o)", t=PACK))
+        nc.sync.dma_start(n4_t[:], n4)
+        nc.sync.dma_start(n5_t[:], n5)
+
+        win_a = [sb.tile([P, WIN], F32, name="win_a%d" % t) for t in range(PACK)]
+        win_b = [sb.tile([P, WIN], F32, name="win_b%d" % t) for t in range(PACK)]
+        for t in range(PACK):
+            nc.vector.memset(win_b[t][:, S:], 0.0)
+            nc.vector.memset(win_a[t][:, S:], 0.0)
+
+        for q in range(4):
+            rows = slice(32 * q, 32 * q + 4)
+            nc.vector.tensor_copy(xs[rows, :].bitcast(I32), xs_in[rows, :].bitcast(I32))
+
+        def dealt(grouped, h):
+            return grouped[:].rearrange("p t m j -> p m j t")[:, 64 * h : 64 * (h + 1)]
+
+        def dealing(raw):
+            return raw.rearrange("p j (m t) -> p m j t", t=PACK)
+
+        def quantize(name, grouped, width):
+            codes = sb.tile([P, width], U32, name=name + "_codes", align_bytes=64)
+            scales = sb.tile([P, width], U8, name=name + "_scales", align_bytes=64)
+            nc.vector.quantize_mx(out=codes[:].bitcast(FP8X4), scales=scales[:], in_=grouped)
+            return codes, scales
+
+        def product(acc, w_q, t, x_q):
+            cols = slice(t * P, (t + 1) * P)
+            nc.tensor.matmul_mx(
+                out=acc,
+                lhsT=w_q[0][:, cols].bitcast(FP8X4),
+                lhsT_scale=w_q[1][:, cols],
+                rhs=x_q[0][:].bitcast(FP8X4),
+                rhs_scale=x_q[1][:],
+                start=True,
+                stop=True,
+            )
+
+        w1_g = sb.tile([P, PACK, P, PACK], BF16, name="w1_g", align_bytes=64)
+        nc.scalar.activation(dealt(w1_g, 0), dealing(w1_raw[0][:]), ACT.Copy)
+        xq_scales = sb.tile([P, S], U8, name="xq_scales", align_bytes=64)
+        nc.vector.tensor_copy(xq_scales[:], xs[:].indirect(offs_t[:]))
+        nc.vector.tensor_copy(dealt(w1_g, 1), dealing(w1_raw[1][:]))
+        w1_q = quantize("w1", w1_g[:].rearrange("p t m j -> p (t m j)"), H)
+        xq_codes = sb.tile([P, S], U32, name="xq_codes", align_bytes=64)
+        nc.vector.tensor_copy(xq_codes[:], xw[:].indirect(offs_t[:]))
+
+        y_ps = [ps.tile([P, S], F32, name="y_ps%d" % t) for t in range(PACK)]
+        for t in range(PACK):
+            product(y_ps[t][:], w1_q, t, (xq_codes, xq_scales))
+        for t in range(PACK):
+            nc.scalar.activation(win_a[t][:, :S], y_ps[t][:], ACT.Tanh, scale=0.5)
+            nc.vector.tensor_scalar(win_b[t][:, :S], y_ps[t][:], gn_t[:, t : t + 1], None, ALU.mult)
+
+        def interleave(name, planes):
+            grouped = sb.tile([P, S, PACK], BF16, name=name + "_g", align_bytes=64)
+            nc.vector.tensor_copy(
+                grouped[:].rearrange("p (c i) t -> p c t i", i=4), planes[:].rearrange("p t (c i) -> p c t i", i=4)
+            )
+            return grouped[:].rearrange("p c t -> p (c t)")
+
+        w2_g = sb.tile([P, PACK, P, PACK], BF16, name="w2_g", align_bytes=64)
+        for h in range(2):
+            nc.vector.tensor_copy(dealt(w2_g, h), dealing(w2_raw[:, :, h * 256 : (h + 1) * 256]))
+
+        g3 = [sb.tile([P, S], F32, name="g3_%d" % t) for t in range(PACK)]
+        z2 = sb.tile([P, PACK, S], BF16, name="z2")
+        for t in range(PACK):
+            nc.scalar.activation(g3[t][:], win_b[t][:].indirect(n3_t[:]), ACT.Copy)
+            nc.vector.tensor_tensor(z2[:, t, :], win_b[t][:, :S], g3[t][:], ALU.subtract)
+
+        g1 = [sb.tile([P, S], F32, name="g1_%d" % t) for t in range(PACK)]
+        for t in range(PACK):
+            nc.scalar.activation(g1[t][:], win_a[t][:].indirect(n1_t[:]), ACT.Copy, bias=0.5, scale=0.5)
+
+        def gate(t):
+            nc.vector.tensor_tensor(win_a[t][:, :S], win_b[t][:, :S], g1[t][:], ALU.mult)
+
+        w2_q = quantize("w2", w2_g[:].rearrange("p t m j -> p (t m j)"), H)
+        z2_g = interleave("z2", z2)
+        gate(0)
+        z2_q = quantize("z2", z2_g, S)
+        for t in range(1, PACK):
+            gate(t)
+
+        b_ps = [ps.tile([P, 2, S], F32, name="b_ps%d" % q) for q in range(2)]
+        for t in range(PACK):
+            product(b_ps[t // 2][:, t % 2, :], w2_q, t, z2_q)
+
+        g2 = [sb.tile([P, S], F32, name="g2_%d" % t) for t in range(PACK)]
+        z = sb.tile([P, PACK, S], BF16, name="z")
+        top = sb.tile([P, PACK], F32, name="top")
+        bias = sb.tile([P, PACK], F32, name="bias")
+        for t in range(PACK):
+            nc.scalar.activation(g2[t][:], win_a[t][:].indirect(n2_t[:]), ACT.Copy)
+
+        def take_b(t):
+            nc.vector.tensor_scalar(
+                win_b[t][:, :S], b_ps[t // 2][:, t % 2, :], 1.0, None, ALU.mult, ALU.max, accum_out=top[:, t : t + 1]
+            )
+
+        def make_bias(q):
+            cols = slice(2 * q, 2 * q + 2)
+            nc.vector.scalar_tensor_tensor(bias[:, cols], top[:, cols], -1.0, tau_t[:, cols], ALU.mult, ALU.mult)
+
+        def make_z(t):
+            nc.vector.tensor_tensor(z[:, t, :], win_a[t][:, :S], g2[t][:], ALU.subtract)
+
+        take_b(0)
+        make_z(0)
+        take_b(1)
+        make_z(1)
+        make_bias(0)
+        make_z(2)
+        make_z(3)
+        z_g = interleave("z", z)
+        take_b(2)
+        z_q = quantize("z", z_g, S)
+        take_b(3)
+        make_bias(1)
+
+        a_ps = [ps.tile([P, 2, S], F32, name="a_ps%d" % q) for q in range(2)]
+        for t in range(PACK):
+            product(a_ps[t // 2][:, t % 2, :], w2_q, t, z_q)
+
+        ea = sb.tile([P, PACK, S], F32, name="ea")
+        for t in range(PACK):
+            nc.scalar.activation(
+                ea[:, t, :], win_b[t][:].indirect(n4_t[:]), ACT.Exp, bias=bias[:, t : t + 1], scale=tau_t[:, t : t + 1]
+            )
+        win_c = [sb.tile([P, WIN], F32, name="win_c%d" % t) for t in range(PACK)]
+        nc.scalar.copy(win_c[2][:], a_ps[1][:].rearrange("p e c -> p (e c)"))
+        root = [win_b[3], win_b[2]]
+        inverse = [sb.tile([P, WIN], F32, name="inverse%d" % q) for q in range(2)]
+        for q in range(2):
+            pair = ea[:, 2 * q : 2 * q + 2, :].rearrange("p e c -> p (e c)")
+            nc.scalar.activation(root[q][:], pair, ACT.Abs_reciprocal_sqrt, bias=0.5, scale=2.0)
+        for q in range(2):
+            nc.scalar.activation(inverse[q][:], root[q][:], ACT.Square)
+
+        diff = [sb.tile([P, S], F32, name="diff%d" % t) for t in range(PACK)]
+        nc.vector.tensor_copy(win_c[0][:], a_ps[0][:].rearrange("p e c -> p (e c)"))
+        for q in range(2):
+            even, odd = win_c[2 * q], win_c[2 * q + 1]
+            nc.vector.tensor_copy(odd[:, :S], even[:, S:])
+            nc.vector.tensor_copy(odd[:, S:], even[:, :S])
+            nc.vector.tensor_tensor(diff[2 * q][:], even[:].indirect(n5_t[:]), odd[:, S:], ALU.subtract)
+            nc.vector.tensor_tensor(diff[2 * q + 1][:], odd[:].indirect(n5_t[:]), even[:, S:], ALU.subtract)
+
+        out_rows = out.rearrange("(p t) c -> p t c", t=PACK)
+        res = [sb.tile([P, S], F32, name="res%d" % t) for t in range(PACK)]
+        for t in range(PACK):
+            cols = slice((t % 2) * S, (t % 2 + 1) * S)
+            nc.vector.scalar_tensor_tensor(res[t][:], diff[t][:], -1.0, inverse[t // 2][:, cols], ALU.mult, ALU.mult)
+            nc.sync.dma_start(out=out_rows[:, t, :], in_=res[t][:])

@@ -1,6 +1,7 @@
 from contextlib import ExitStack
 
 import concourse.mybir as mybir
+from concourse.masks import make_identity
 
 K, T, S, H = 512, 2048, 256, 512
 FLOPS = 3 * 2 * 512 * 512 * 256
@@ -27,6 +28,7 @@ def tile_picked_tieqxbhopgdif_none_p_kernel(
     with ExitStack() as ctx:
         lists = ctx.enter_context(tc.tile_pool(name="lists", bufs=1))
         sb = ctx.enter_context(tc.tile_pool(name="sb", bufs=1))
+        reuse = ctx.enter_context(tc.tile_pool(name="reuse", bufs=1))
         ps = ctx.enter_context(tc.psum_pool(name="ps", bufs=1))
 
         def list_tile(name):
@@ -37,8 +39,8 @@ def tile_picked_tieqxbhopgdif_none_p_kernel(
         xw = sb.tile([P, T], U32, name="xw")
         xs = sb.tile([P, T], U8, name="xs")
         xs_in = sb.tile([P, T], U8, name="xs_in")
-        w1_raw = [sb.tile([P, PACK, H // 2], F32, name="w1_raw%d" % h) for h in range(2)]
-        w2_raw = sb.tile([P, PACK, H], F32, name="w2_raw")
+        w1_raw = sb.tile([P, PACK, H], F32, name="w1_raw")
+        w2_raw = reuse.tile([P, PACK, H], F32, name="w2_raw", offset=0)
         gn_t = sb.tile([P, PACK], F32, name="gn")
         tau_t = sb.tile([P, PACK], F32, name="tau")
 
@@ -50,37 +52,38 @@ def tile_picked_tieqxbhopgdif_none_p_kernel(
                 out=xs_in[32 * q : 32 * q + 4, :].bitcast(I32), in_=x_scales[0, 4 * q : 4 * q + 4, :].bitcast(I32)
             )
 
-        nc.sync.dma_start(out=w1_raw[0][:], in_=w1_rows[:, :, :256])
-        for q in range(3):
-            load_scale_rows(nc.scalar, q)
-        load_scale_rows(nc.sync, 3)
-        nc.sync.dma_start(out=w1_raw[1][:], in_=w1_rows[:, :, 256:])
+        for q in range(4):
+            load_scale_rows(nc.scalar if q < 2 else nc.sync, q)
+        nc.sync.dma_start(out=w1_raw[:], in_=w1_rows)
         nc.sync.dma_start(offs_t[:], offs)
         nc.sync.dma_start(out=xw[:].bitcast(I32), in_=x_words[0].rearrange("p c r -> p (c r)").bitcast(I32))
-        nc.sync.dma_start(out=gn_t[:], in_=gn.rearrange("(p t) o -> p (t o)", t=PACK))
+        gn_run = sb.tile([P, 16], F32, name="gn_run")
+        nc.sync.dma_start(out=gn_run[:], in_=gn.rearrange("(u w) o -> u o w", w=16).to_broadcast([32, 4, 16]))
         nc.sync.dma_start(n3_t[:], n3)
-        nc.sync.dma_start(out=w2_raw[:], in_=w2.rearrange("(p j) c -> p j c", j=PACK))
+        w2_rows = w2.rearrange("(u j v) c -> j u v c", j=PACK, v=4)
+        for j in range(PACK):
+            nc.sync.dma_start(out=w2_raw[:, j, :], in_=w2_rows[j])
         nc.sync.dma_start(n1_t[:], n1)
         nc.sync.dma_start(n2_t[:], n2)
-        nc.sync.dma_start(out=tau_t[:], in_=tau.rearrange("(p t) o -> p (t o)", t=PACK))
+        with nc.allow_non_contiguous_dma(reason="one rate a partition and tile"):
+            nc.sync.dma_start(out=tau_t[:], in_=tau.rearrange("(t p) o -> p (t o)", p=P))
         nc.sync.dma_start(n4_t[:], n4)
         nc.sync.dma_start(n5_t[:], n5)
 
-        win_a = [sb.tile([P, WIN], F32, name="win_a%d" % t) for t in range(PACK)]
-        win_b = [sb.tile([P, WIN], F32, name="win_b%d" % t) for t in range(PACK)]
+        win = [sb.tile([P, WIN], F32, name="win%d" % t) for t in range(PACK)]
+        yg = [sb.tile([P, WIN], F32, name="yg%d" % t) for t in range(PACK)]
         for t in range(PACK):
-            nc.vector.memset(win_b[t][:, S:], 0.0)
-            nc.vector.memset(win_a[t][:, S:], 0.0)
+            nc.vector.memset(yg[t][:, S:], 0.0)
+            nc.vector.memset(win[t][:, S:], 0.0)
 
         for q in range(4):
             rows = slice(32 * q, 32 * q + 4)
             nc.vector.tensor_copy(xs[rows, :].bitcast(I32), xs_in[rows, :].bitcast(I32))
 
-        def dealt(grouped, h):
-            return grouped[:].rearrange("p t m j -> p m j t")[:, 64 * h : 64 * (h + 1)]
-
-        def dealing(raw):
-            return raw.rearrange("p j (m t) -> p m j t", t=PACK)
+        eye = sb.tile([P, P], F32, name="eye")
+        make_identity(nc, eye[:])
+        own = sb.tile([P, 4], F32, name="own")
+        nc.vector.tensor_reduce(own[:], eye[:].rearrange("p (u v) -> p v u", v=4), mybir.AxisListType.X, ALU.add)
 
         def quantize(name, grouped, width):
             codes = sb.tile([P, width], U32, name=name + "_codes", align_bytes=64)
@@ -88,62 +91,81 @@ def tile_picked_tieqxbhopgdif_none_p_kernel(
             nc.vector.quantize_mx(out=codes[:].bitcast(FP8X4), scales=scales[:], in_=grouped)
             return codes, scales
 
-        def product(acc, w_q, t, x_q):
+        def product(acc, w_q, t, x_q, places=slice(0, S)):
             cols = slice(t * P, (t + 1) * P)
             nc.tensor.matmul_mx(
                 out=acc,
                 lhsT=w_q[0][:, cols].bitcast(FP8X4),
                 lhsT_scale=w_q[1][:, cols],
-                rhs=x_q[0][:].bitcast(FP8X4),
-                rhs_scale=x_q[1][:],
+                rhs=x_q[0][:, places].bitcast(FP8X4),
+                rhs_scale=x_q[1][:, places],
                 start=True,
                 stop=True,
             )
 
         w1_g = sb.tile([P, PACK, P, PACK], BF16, name="w1_g", align_bytes=64)
-        nc.scalar.activation(dealt(w1_g, 0), dealing(w1_raw[0][:]), ACT.Copy)
+        w1_to = w1_g[:].rearrange("p t (u v) j -> p t u j v", v=4)
+        w1_from = w1_raw[:].rearrange("p j (u t v) -> p t u j v", t=PACK, v=4)
+        for t in range(2):
+            nc.scalar.activation(w1_to[:, t], w1_from[:, t], ACT.Copy)
         xq_scales = sb.tile([P, S], U8, name="xq_scales", align_bytes=64)
         nc.vector.tensor_copy(xq_scales[:], xs[:].indirect(offs_t[:]))
-        nc.vector.tensor_copy(dealt(w1_g, 1), dealing(w1_raw[1][:]))
-        w1_q = quantize("w1", w1_g[:].rearrange("p t m j -> p (t m j)"), H)
+        nc.vector.tensor_copy(w1_to[:, 2:], w1_from[:, 2:])
+        w1_q = (sb.tile([P, H], U32, name="w1_codes", align_bytes=64), sb.tile([P, H], U8, name="w1_scales", align_bytes=64))
+        for lo in (2, 0):
+            cols = slice(P * lo, P * (lo + 2))
+            nc.vector.quantize_mx(
+                out=w1_q[0][:, cols].bitcast(FP8X4),
+                scales=w1_q[1][:, cols],
+                in_=w1_g[:, lo : lo + 2].rearrange("p t m j -> p (t m j)"),
+            )
         xq_codes = sb.tile([P, S], U32, name="xq_codes", align_bytes=64)
         nc.vector.tensor_copy(xq_codes[:], xw[:].indirect(offs_t[:]))
 
-        y_ps = [ps.tile([P, S], F32, name="y_ps%d" % t) for t in range(PACK)]
+        gn_kept = sb.tile([P, PACK, 4], F32, name="gn_kept")
+        nc.vector.tensor_tensor(
+            gn_kept[:],
+            gn_run[:].rearrange("p (t v) -> p t v", v=4),
+            own[:].unsqueeze(1).to_broadcast([P, PACK, 4]),
+            ALU.mult,
+        )
+        nc.vector.tensor_reduce(gn_t[:], gn_kept[:], mybir.AxisListType.X, ALU.add)
+
+        y_ps = [ps.tile([P, S], F32, name="y_ps", tag="y_ps%d" % t) for t in range(PACK)]
         for t in range(PACK):
             product(y_ps[t][:], w1_q, t, (xq_codes, xq_scales))
         for t in range(PACK):
-            nc.scalar.activation(win_a[t][:, :S], y_ps[t][:], ACT.Tanh, scale=0.5)
-            nc.vector.tensor_scalar(win_b[t][:, :S], y_ps[t][:], gn_t[:, t : t + 1], None, ALU.mult)
+            nc.scalar.activation(win[t][:, :S], y_ps[t][:], ACT.Tanh, scale=0.5)
+            nc.vector.tensor_scalar(yg[t][:, :S], y_ps[t][:], gn_t[:, t : t + 1], None, ALU.mult)
 
-        def interleave(name, planes):
-            grouped = sb.tile([P, S, PACK], BF16, name=name + "_g", align_bytes=64)
-            nc.vector.tensor_copy(
-                grouped[:].rearrange("p (c i) t -> p c t i", i=4), planes[:].rearrange("p t (c i) -> p c t i", i=4)
-            )
-            return grouped[:].rearrange("p c t -> p (c t)")
-
-        w2_g = sb.tile([P, PACK, P, PACK], BF16, name="w2_g", align_bytes=64)
+        w2_g = sb.tile([P, H, PACK], BF16, name="w2_g", align_bytes=64)
+        w2_to = w2_g[:].rearrange("p (c i) j -> p c j i", i=4)
+        w2_from = w2_raw[:].rearrange("p j (c i) -> p c j i", i=4)
         for h in range(2):
-            nc.vector.tensor_copy(dealt(w2_g, h), dealing(w2_raw[:, :, h * 256 : (h + 1) * 256]))
+            nc.vector.tensor_copy(w2_to[:, 64 * h : 64 * (h + 1)], w2_from[:, 64 * h : 64 * (h + 1)])
 
         g3 = [sb.tile([P, S], F32, name="g3_%d" % t) for t in range(PACK)]
-        z2 = sb.tile([P, PACK, S], BF16, name="z2")
+        z2 = reuse.tile([P, PACK, S], BF16, name="z2", offset=0)
         for t in range(PACK):
-            nc.scalar.activation(g3[t][:], win_b[t][:].indirect(n3_t[:]), ACT.Copy)
-            nc.vector.tensor_tensor(z2[:, t, :], win_b[t][:, :S], g3[t][:], ALU.subtract)
+            nc.scalar.activation(g3[t][:], yg[t][:].indirect(n3_t[:]), ACT.Copy)
+            nc.vector.tensor_tensor(z2[:, t, :], yg[t][:, :S], g3[t][:], ALU.subtract)
 
-        g1 = [sb.tile([P, S], F32, name="g1_%d" % t) for t in range(PACK)]
+        g1 = [reuse.tile([P, S], F32, name="g1_%d" % t, offset=2048 + 1024 * t) for t in range(PACK)]
         for t in range(PACK):
-            nc.scalar.activation(g1[t][:], win_a[t][:].indirect(n1_t[:]), ACT.Copy, bias=0.5, scale=0.5)
+            nc.scalar.activation(g1[t][:], win[t][:].indirect(n1_t[:]), ACT.Copy, bias=0.5, scale=0.5)
+
+        st = sb.tile([P, PACK, S], F32, name="st")
 
         def gate(t):
-            nc.vector.tensor_tensor(win_a[t][:, :S], win_b[t][:, :S], g1[t][:], ALU.mult)
+            nc.vector.tensor_tensor(st[:, t, :], yg[t][:, :S], g1[t][:], ALU.mult)
 
-        w2_q = quantize("w2", w2_g[:].rearrange("p t m j -> p (t m j)"), H)
-        z2_g = interleave("z2", z2)
+        w2_q = quantize("w2", w2_g[:].rearrange("p c j -> p (c j)"), H)
+        z2_g = sb.tile([P, S, PACK], BF16, name="z2_g", align_bytes=64)
+        nc.vector.tensor_copy(
+            z2_g[:].rearrange("p (c i) t -> p c t i", i=4), z2[:].rearrange("p t (c i) -> p c t i", i=4)
+        )
         gate(0)
-        z2_q = quantize("z2", z2_g, S)
+        z2_q = quantize("z2", z2_g[:].rearrange("p c t -> p (c t)"), S)
         for t in range(1, PACK):
             gate(t)
 
@@ -151,69 +173,92 @@ def tile_picked_tieqxbhopgdif_none_p_kernel(
         for t in range(PACK):
             product(b_ps[t // 2][:, t % 2, :], w2_q, t, z2_q)
 
-        g2 = [sb.tile([P, S], F32, name="g2_%d" % t) for t in range(PACK)]
-        z = sb.tile([P, PACK, S], BF16, name="z")
+        g2_at = (7168, 4608, 5632, 7168)
+        g2 = [reuse.tile([P, PACK, 64], F32, name="g2_%d" % q, offset=g2_at[q]) for q in range(4)]
+        for q in range(4):
+            for t in range(PACK):
+                nc.scalar.activation(g2[q][:, t, :], st[:, t, :].indirect(n2_t[:, 4 * q : 4 * (q + 1)]), ACT.Copy)
+
         top = sb.tile([P, PACK], F32, name="top")
         bias = sb.tile([P, PACK], F32, name="bias")
-        for t in range(PACK):
-            nc.scalar.activation(g2[t][:], win_a[t][:].indirect(n2_t[:]), ACT.Copy)
+        z_g = sb.tile([P, S, PACK], BF16, name="z_g", align_bytes=64)
+        z_codes = sb.tile([P, S], U32, name="z_codes", align_bytes=64)
+        z_scales = sb.tile([P, S], U8, name="z_scales", align_bytes=64)
+        a_ps = [[ps.tile([P, 2, P], F32, name="a_ps", tag="y_ps%d" % (2 * h + q)) for q in range(2)] for h in range(2)]
+        win_c = [sb.tile([P, WIN], F32, name="win_c%d" % t) for t in range(PACK)]
 
         def take_b(t):
             nc.vector.tensor_scalar(
-                win_b[t][:, :S], b_ps[t // 2][:, t % 2, :], 1.0, None, ALU.mult, ALU.max, accum_out=top[:, t : t + 1]
+                win[t][:, :S], b_ps[t // 2][:, t % 2, :], 1.0, None, ALU.mult, ALU.max, accum_out=top[:, t : t + 1]
             )
 
         def make_bias(q):
             cols = slice(2 * q, 2 * q + 2)
             nc.vector.scalar_tensor_tensor(bias[:, cols], top[:, cols], -1.0, tau_t[:, cols], ALU.mult, ALU.mult)
 
-        def make_z(t):
-            nc.vector.tensor_tensor(z[:, t, :], win_a[t][:, :S], g2[t][:], ALU.subtract)
+        def make_z(q):
+            places = slice(64 * q, 64 * (q + 1))
+            nc.vector.tensor_tensor(
+                z_g[:, places, :].rearrange("p (c i) t -> p c t i", i=4),
+                st[:, :, places].rearrange("p t (c i) -> p c t i", i=4),
+                g2[q][:].rearrange("p t (c i) -> p c t i", i=4),
+                ALU.subtract,
+            )
+
+        def make_a(h):
+            places = slice(128 * h, 128 * (h + 1))
+            nc.vector.quantize_mx(
+                out=z_codes[:, places].bitcast(FP8X4),
+                scales=z_scales[:, places],
+                in_=z_g[:, places, :].rearrange("p c t -> p (c t)"),
+            )
+            for t in range(PACK):
+                product(a_ps[h][t // 2][:, t % 2, :], w2_q, t, (z_codes, z_scales), places)
+
+        def take_a(h, q):
+            pair = win_c[2 * q][:].rearrange("p (e c) -> p e c", e=2)
+            nc.vector.tensor_copy(pair[:, :, 128 * h : 128 * (h + 1)], a_ps[h][q][:])
 
         take_b(0)
         make_z(0)
         take_b(1)
         make_z(1)
         make_bias(0)
-        make_z(2)
-        make_z(3)
-        z_g = interleave("z", z)
         take_b(2)
-        z_q = quantize("z", z_g, S)
+        make_a(0)
+        make_z(2)
+        take_a(0, 0)
+        make_z(3)
         take_b(3)
+        make_a(1)
         make_bias(1)
-
-        a_ps = [ps.tile([P, 2, S], F32, name="a_ps%d" % q) for q in range(2)]
-        for t in range(PACK):
-            product(a_ps[t // 2][:, t % 2, :], w2_q, t, z_q)
+        take_a(0, 1)
+        take_a(1, 0)
+        take_a(1, 1)
 
         ea = sb.tile([P, PACK, S], F32, name="ea")
         for t in range(PACK):
             nc.scalar.activation(
-                ea[:, t, :], win_b[t][:].indirect(n4_t[:]), ACT.Exp, bias=bias[:, t : t + 1], scale=tau_t[:, t : t + 1]
+                ea[:, t, :], win[t][:].indirect(n4_t[:]), ACT.Exp, bias=bias[:, t : t + 1], scale=tau_t[:, t : t + 1]
             )
-        win_c = [sb.tile([P, WIN], F32, name="win_c%d" % t) for t in range(PACK)]
-        nc.scalar.copy(win_c[2][:], a_ps[1][:].rearrange("p e c -> p (e c)"))
-        root = [win_b[3], win_b[2]]
-        inverse = [sb.tile([P, WIN], F32, name="inverse%d" % q) for q in range(2)]
+        root = [win[3], win[2]]
+        inverse = [sb.tile([P, S], F32, name="inverse%d" % t) for t in range(PACK)]
         for q in range(2):
             pair = ea[:, 2 * q : 2 * q + 2, :].rearrange("p e c -> p (e c)")
             nc.scalar.activation(root[q][:], pair, ACT.Abs_reciprocal_sqrt, bias=0.5, scale=2.0)
-        for q in range(2):
-            nc.scalar.activation(inverse[q][:], root[q][:], ACT.Square)
+        for t in range(PACK):
+            nc.scalar.activation(inverse[t][:], root[t // 2][:, (t % 2) * S : (t % 2 + 1) * S], ACT.Square)
 
         diff = [sb.tile([P, S], F32, name="diff%d" % t) for t in range(PACK)]
-        nc.vector.tensor_copy(win_c[0][:], a_ps[0][:].rearrange("p e c -> p (e c)"))
         for q in range(2):
             even, odd = win_c[2 * q], win_c[2 * q + 1]
-            nc.vector.tensor_copy(odd[:, :S], even[:, S:])
             nc.vector.tensor_copy(odd[:, S:], even[:, :S])
+            nc.vector.tensor_copy(odd[:, :S], even[:, S:])
             nc.vector.tensor_tensor(diff[2 * q][:], even[:].indirect(n5_t[:]), odd[:, S:], ALU.subtract)
             nc.vector.tensor_tensor(diff[2 * q + 1][:], odd[:].indirect(n5_t[:]), even[:, S:], ALU.subtract)
 
-        out_rows = out.rearrange("(p t) c -> p t c", t=PACK)
+        out_rows = out.rearrange("(t p) c -> p t c", p=P)
         res = [sb.tile([P, S], F32, name="res%d" % t) for t in range(PACK)]
         for t in range(PACK):
-            cols = slice((t % 2) * S, (t % 2 + 1) * S)
-            nc.vector.scalar_tensor_tensor(res[t][:], diff[t][:], -1.0, inverse[t // 2][:, cols], ALU.mult, ALU.mult)
+            nc.vector.scalar_tensor_tensor(res[t][:], diff[t][:], -1.0, inverse[t][:], ALU.mult, ALU.mult)
             nc.sync.dma_start(out=out_rows[:, t, :], in_=res[t][:])

@@ -71,9 +71,8 @@ def tile_picked_tieqxbhopgdif_none_p_kernel(
         nc.sync.dma_start(n5_t[:], n5)
 
         win = [sb.tile([P, WIN], F32, name="win%d" % t) for t in range(PACK)]
-        yg = [sb.tile([P, WIN], F32, name="yg%d" % t) for t in range(PACK)]
+        yg = sb.tile([P, PACK, S], F32, name="yg")
         for t in range(PACK):
-            nc.vector.memset(yg[t][:, S:], 0.0)
             nc.vector.memset(win[t][:, S:], 0.0)
 
         for q in range(4):
@@ -136,7 +135,7 @@ def tile_picked_tieqxbhopgdif_none_p_kernel(
             product(y_ps[t][:], w1_q, t, (xq_codes, xq_scales))
         for t in range(PACK):
             nc.scalar.activation(win[t][:, :S], y_ps[t][:], ACT.Tanh, scale=0.5)
-            nc.vector.tensor_scalar(yg[t][:, :S], y_ps[t][:], gn_t[:, t : t + 1], None, ALU.mult)
+            nc.vector.tensor_scalar(yg[:, t, :], y_ps[t][:], gn_t[:, t : t + 1], None, ALU.mult)
 
         w2_g = sb.tile([P, H, PACK], BF16, name="w2_g", align_bytes=64)
         w2_to = w2_g[:].rearrange("p (c i) j -> p c j i", i=4)
@@ -144,11 +143,12 @@ def tile_picked_tieqxbhopgdif_none_p_kernel(
         for h in range(2):
             nc.vector.tensor_copy(w2_to[:, 64 * h : 64 * (h + 1)], w2_from[:, 64 * h : 64 * (h + 1)])
 
-        g3 = [sb.tile([P, S], F32, name="g3_%d" % t) for t in range(PACK)]
-        z2 = reuse.tile([P, PACK, S], BF16, name="z2", offset=0)
+        g3 = sb.tile([P, PACK, S], F32, name="g3")
         for t in range(PACK):
-            nc.scalar.activation(g3[t][:], yg[t][:].indirect(n3_t[:]), ACT.Copy)
-            nc.vector.tensor_tensor(z2[:, t, :], yg[t][:, :S], g3[t][:], ALU.subtract)
+            for q in range(4):
+                nc.scalar.activation(
+                    g3[:, t, 64 * q : 64 * (q + 1)], yg[:, t, :].indirect(n3_t[:, 4 * q : 4 * (q + 1)]), ACT.Copy
+                )
 
         g1 = [reuse.tile([P, S], F32, name="g1_%d" % t, offset=2048 + 1024 * t) for t in range(PACK)]
         for t in range(PACK):
@@ -157,13 +157,18 @@ def tile_picked_tieqxbhopgdif_none_p_kernel(
         st = sb.tile([P, PACK, S], F32, name="st")
 
         def gate(t):
-            nc.vector.tensor_tensor(st[:, t, :], yg[t][:, :S], g1[t][:], ALU.mult)
+            nc.vector.tensor_tensor(st[:, t, :], yg[:, t, :], g1[t][:], ALU.mult)
 
         w2_q = quantize("w2", w2_g[:].rearrange("p c j -> p (c j)"), H)
-        z2_g = sb.tile([P, S, PACK], BF16, name="z2_g", align_bytes=64)
-        nc.vector.tensor_copy(
-            z2_g[:].rearrange("p (c i) t -> p c t i", i=4), z2[:].rearrange("p t (c i) -> p c t i", i=4)
-        )
+        z2_g = reuse.tile([P, S, PACK], BF16, name="z2_g", align_bytes=64, offset=0)
+        for h in range(2):
+            places = slice(P * h, P * (h + 1))
+            nc.vector.tensor_tensor(
+                z2_g[:, places, :].rearrange("p (c i) t -> p c t i", i=4),
+                yg[:, :, places].rearrange("p t (c i) -> p c t i", i=4),
+                g3[:, :, places].rearrange("p t (c i) -> p c t i", i=4),
+                ALU.subtract,
+            )
         gate(0)
         z2_q = quantize("z2", z2_g[:].rearrange("p c t -> p (c t)"), S)
         for t in range(1, PACK):
@@ -241,13 +246,18 @@ def tile_picked_tieqxbhopgdif_none_p_kernel(
             nc.scalar.activation(
                 ea[:, t, :], win[t][:].indirect(n4_t[:]), ACT.Exp, bias=bias[:, t : t + 1], scale=tau_t[:, t : t + 1]
             )
-        root = [win[3], win[2]]
-        inverse = [sb.tile([P, S], F32, name="inverse%d" % t) for t in range(PACK)]
-        for q in range(2):
-            pair = ea[:, 2 * q : 2 * q + 2, :].rearrange("p e c -> p (e c)")
-            nc.scalar.activation(root[q][:], pair, ACT.Abs_reciprocal_sqrt, bias=0.5, scale=2.0)
-        for t in range(PACK):
-            nc.scalar.activation(inverse[t][:], root[t // 2][:, (t % 2) * S : (t % 2 + 1) * S], ACT.Square)
+        quad = sb.tile([P, 2, S], F32, name="quad")
+        for t in range(2):
+            nc.vector.scalar_tensor_tensor(quad[:, t, :], ea[:, t, :], 0.5, ea[:, t, :], ALU.add, ALU.mult)
+        nc.scalar.activation(win[3][:], quad[:].rearrange("p e c -> p (e c)"), ACT.Abs_reciprocal_sqrt, bias=0.25, scale=4.0)
+        nc.scalar.activation(
+            win[2][:], ea[:, 2:, :].rearrange("p e c -> p (e c)"), ACT.Abs_reciprocal_sqrt, bias=0.5, scale=2.0
+        )
+        inverse = [win[3][:, :S], win[3][:, S:]]
+        for t in range(2):
+            square = sb.tile([P, S], F32, name="square%d" % t)
+            nc.scalar.activation(square[:], win[2][:, t * S : (t + 1) * S], ACT.Square)
+            inverse.append(square[:])
 
         diff = [sb.tile([P, S], F32, name="diff%d" % t) for t in range(PACK)]
         for q in range(2):
@@ -260,5 +270,5 @@ def tile_picked_tieqxbhopgdif_none_p_kernel(
         out_rows = out.rearrange("(t p) c -> p t c", p=P)
         res = [sb.tile([P, S], F32, name="res%d" % t) for t in range(PACK)]
         for t in range(PACK):
-            nc.vector.scalar_tensor_tensor(res[t][:], diff[t][:], -1.0, inverse[t][:], ALU.mult, ALU.mult)
+            nc.vector.scalar_tensor_tensor(res[t][:], diff[t][:], -1.0, inverse[t], ALU.mult, ALU.mult)
             nc.sync.dma_start(out=out_rows[:, t, :], in_=res[t][:])

from contextlib import ExitStack

import concourse.mybir as mybir
from concourse.masks import make_identity

K, T, S, H = 512, 2048, 256, 512
FLOPS = 3 * 2 * 512 * 512 * 256

F32 = mybir.dt.float32
BF16 = mybir.dt.bfloat16
I32 = mybir.dt.int32
U32 = mybir.dt.uint32
U16 = mybir.dt.uint16
U8 = mybir.dt.uint8
FP8X4 = mybir.dt.float8_e4m3fn_x4
ALU = mybir.AluOpType
ACT = mybir.ActivationFunctionType

P = 128
PACK = 4
WIN = 2 * S


def tile_picked_tieqxbhopgdif_none_p_kernel(
    tc, x_words, x_scales, w1, gn, w2, tau, offs, n1, n2, n3, n4, n5, out
):
    nc = tc.nc
    with ExitStack() as ctx:
        lists = ctx.enter_context(tc.tile_pool(name="lists", bufs=1))
        sb = ctx.enter_context(tc.tile_pool(name="sb", bufs=1))
        reuse = ctx.enter_context(tc.tile_pool(name="reuse", bufs=1))
        ps = ctx.enter_context(tc.psum_pool(name="ps", bufs=1))

        def list_tile(name):
            return lists.tile([P, S // 16], U16, name=name)

        offs_t, n1_t, n2_t, n3_t, n4_t, n5_t = [list_tile(n) for n in ("offs", "n1", "n2", "n3", "n4", "n5")]

        xw = sb.tile([P, T], U32, name="xw")
        xs = sb.tile([P, T], U8, name="xs")
        xs_in = sb.tile([P, T], U8, name="xs_in")
        w1_raw = sb.tile([P, PACK, H], F32, name="w1_raw")
        w2_raw = reuse.tile([P, PACK, H], F32, name="w2_raw", offset=0)
        gn_t = sb.tile([P, PACK], F32, name="gn")
        tau_t = sb.tile([P, PACK], F32, name="tau")

        nc.vector.memset(xs[:].bitcast(I32), 0)
        w1_rows = w1.rearrange("(p j) c -> p j c", j=PACK)

        def load_scale_rows(queue, q):
            queue.dma_start(
                out=xs_in[32 * q : 32 * q + 4, :].bitcast(I32), in_=x_scales[0, 4 * q : 4 * q + 4, :].bitcast(I32)
            )

        for q in range(4):
            load_scale_rows(nc.scalar if q < 2 else nc.sync, q)
        nc.sync.dma_start(out=w1_raw[:], in_=w1_rows)
        nc.sync.dma_start(offs_t[:], offs)
        nc.sync.dma_start(out=xw[:].bitcast(I32), in_=x_words[0].rearrange("p c r -> p (c r)").bitcast(I32))
        gn_run = sb.tile([P, 16], F32, name="gn_run")
        nc.sync.dma_start(out=gn_run[:], in_=gn.rearrange("(u w) o -> u o w", w=16).to_broadcast([32, 4, 16]))
        nc.sync.dma_start(n3_t[:], n3)
        w2_rows = w2.rearrange("(u j v) c -> j u v c", j=PACK, v=4)
        for j in range(PACK):
            nc.sync.dma_start(out=w2_raw[:, j, :], in_=w2_rows[j])
        nc.sync.dma_start(n1_t[:], n1)
        nc.sync.dma_start(n2_t[:], n2)
        with nc.allow_non_contiguous_dma(reason="one rate a partition and tile"):
            nc.sync.dma_start(out=tau_t[:], in_=tau.rearrange("(t p) o -> p (t o)", p=P))
        nc.sync.dma_start(n4_t[:], n4)
        nc.sync.dma_start(n5_t[:], n5)

        win = [sb.tile([P, WIN], F32, name="win%d" % t) for t in range(PACK)]
        yg = sb.tile([P, PACK, S], F32, name="yg")
        for t in range(PACK):
            nc.vector.memset(win[t][:, S:], 0.0)

        for q in range(4):
            rows = slice(32 * q, 32 * q + 4)
            nc.vector.tensor_copy(xs[rows, :].bitcast(I32), xs_in[rows, :].bitcast(I32))

        eye = sb.tile([P, P], F32, name="eye")
        make_identity(nc, eye[:])
        own = sb.tile([P, 4], F32, name="own")
        nc.vector.tensor_reduce(own[:], eye[:].rearrange("p (u v) -> p v u", v=4), mybir.AxisListType.X, ALU.add)

        def quantize(name, grouped, width):
            codes = sb.tile([P, width], U32, name=name + "_codes", align_bytes=64)
            scales = sb.tile([P, width], U8, name=name + "_scales", align_bytes=64)
            nc.vector.quantize_mx(out=codes[:].bitcast(FP8X4), scales=scales[:], in_=grouped)
            return codes, scales

        def product(acc, w_q, t, x_q, places=slice(0, S)):
            cols = slice(t * P, (t + 1) * P)
            nc.tensor.matmul_mx(
                out=acc,
                lhsT=w_q[0][:, cols].bitcast(FP8X4),
                lhsT_scale=w_q[1][:, cols],
                rhs=x_q[0][:, places].bitcast(FP8X4),
                rhs_scale=x_q[1][:, places],
                start=True,
                stop=True,
            )

        w1_g = sb.tile([P, PACK, P, PACK], BF16, name="w1_g", align_bytes=64)
        w1_to = w1_g[:].rearrange("p t (u v) j -> p t u j v", v=4)
        w1_from = w1_raw[:].rearrange("p j (u t v) -> p t u j v", t=PACK, v=4)
        for t in range(2):
            nc.scalar.activation(w1_to[:, t], w1_from[:, t], ACT.Copy)
        xq_scales = sb.tile([P, S], U8, name="xq_scales", align_bytes=64)
        nc.vector.tensor_copy(xq_scales[:], xs[:].indirect(offs_t[:]))
        nc.vector.tensor_copy(w1_to[:, 2:], w1_from[:, 2:])
        w1_q = (sb.tile([P, H], U32, name="w1_codes", align_bytes=64), sb.tile([P, H], U8, name="w1_scales", align_bytes=64))
        for lo in (2, 0):
            cols = slice(P * lo, P * (lo + 2))
            nc.vector.quantize_mx(
                out=w1_q[0][:, cols].bitcast(FP8X4),
                scales=w1_q[1][:, cols],
                in_=w1_g[:, lo : lo + 2].rearrange("p t m j -> p (t m j)"),
            )
        xq_codes = sb.tile([P, S], U32, name="xq_codes", align_bytes=64)
        nc.vector.tensor_copy(xq_codes[:], xw[:].indirect(offs_t[:]))

        gn_kept = sb.tile([P, PACK, 4], F32, name="gn_kept")
        nc.vector.tensor_tensor(
            gn_kept[:],
            gn_run[:].rearrange("p (t v) -> p t v", v=4),
            own[:].unsqueeze(1).to_broadcast([P, PACK, 4]),
            ALU.mult,
        )
        nc.vector.tensor_reduce(gn_t[:], gn_kept[:], mybir.AxisListType.X, ALU.add)

        y_ps = [ps.tile([P, S], F32, name="y_ps", tag="y_ps%d" % t) for t in range(PACK)]
        for t in range(PACK):
            product(y_ps[t][:], w1_q, t, (xq_codes, xq_scales))
        for t in range(PACK):
            nc.scalar.activation(win[t][:, :S], y_ps[t][:], ACT.Tanh, scale=0.5)
            nc.vector.tensor_scalar(yg[:, t, :], y_ps[t][:], gn_t[:, t : t + 1], None, ALU.mult)

        w2_g = sb.tile([P, H, PACK], BF16, name="w2_g", align_bytes=64)
        w2_to = w2_g[:].rearrange("p (c i) j -> p c j i", i=4)
        w2_from = w2_raw[:].rearrange("p j (c i) -> p c j i", i=4)
        for h in range(2):
            nc.vector.tensor_copy(w2_to[:, 64 * h : 64 * (h + 1)], w2_from[:, 64 * h : 64 * (h + 1)])

        g3 = sb.tile([P, PACK, S], F32, name="g3")
        for t in range(PACK):
            for q in range(4):
                nc.scalar.activation(
                    g3[:, t, 64 * q : 64 * (q + 1)], yg[:, t, :].indirect(n3_t[:, 4 * q : 4 * (q + 1)]), ACT.Copy
                )

        g1 = [reuse.tile([P, S], F32, name="g1_%d" % t, offset=2048 + 1024 * t) for t in range(PACK)]
        for t in range(PACK):
            nc.scalar.activation(g1[t][:], win[t][:].indirect(n1_t[:]), ACT.Copy, bias=0.5, scale=0.5)

        st = sb.tile([P, PACK, S], F32, name="st")

        def gate(t):
            nc.vector.tensor_tensor(st[:, t, :], yg[:, t, :], g1[t][:], ALU.mult)

        w2_q = quantize("w2", w2_g[:].rearrange("p c j -> p (c j)"), H)
        z2_g = reuse.tile([P, S, PACK], BF16, name="z2_g", align_bytes=64, offset=0)
        for h in range(2):
            places = slice(P * h, P * (h + 1))
            nc.vector.tensor_tensor(
                z2_g[:, places, :].rearrange("p (c i) t -> p c t i", i=4),
                yg[:, :, places].rearrange("p t (c i) -> p c t i", i=4),
                g3[:, :, places].rearrange("p t (c i) -> p c t i", i=4),
                ALU.subtract,
            )
        gate(0)
        z2_q = quantize("z2", z2_g[:].rearrange("p c t -> p (c t)"), S)
        for t in range(1, PACK):
            gate(t)

        b_ps = [ps.tile([P, 2, S], F32, name="b_ps%d" % q) for q in range(2)]
        for t in range(PACK):
            product(b_ps[t // 2][:, t % 2, :], w2_q, t, z2_q)

        g2_at = (7168, 4608, 5632, 7168)
        g2 = [reuse.tile([P, PACK, 64], F32, name="g2_%d" % q, offset=g2_at[q]) for q in range(4)]
        for q in range(4):
            for t in range(PACK):
                nc.scalar.activation(g2[q][:, t, :], st[:, t, :].indirect(n2_t[:, 4 * q : 4 * (q + 1)]), ACT.Copy)

        top = sb.tile([P, PACK], F32, name="top")
        bias = sb.tile([P, PACK], F32, name="bias")
        z_g = sb.tile([P, S, PACK], BF16, name="z_g", align_bytes=64)
        z_codes = sb.tile([P, S], U32, name="z_codes", align_bytes=64)
        z_scales = sb.tile([P, S], U8, name="z_scales", align_bytes=64)
        a_ps = [[ps.tile([P, 2, P], F32, name="a_ps", tag="y_ps%d" % (2 * h + q)) for q in range(2)] for h in range(2)]
        win_c = [sb.tile([P, WIN], F32, name="win_c%d" % t) for t in range(PACK)]

        def take_b(t):
            nc.vector.tensor_scalar(
                win[t][:, :S], b_ps[t // 2][:, t % 2, :], 1.0, None, ALU.mult, ALU.max, accum_out=top[:, t : t + 1]
            )

        def make_bias(q):
            cols = slice(2 * q, 2 * q + 2)
            nc.vector.scalar_tensor_tensor(bias[:, cols], top[:, cols], -1.0, tau_t[:, cols], ALU.mult, ALU.mult)

        def make_z(q):
            places = slice(64 * q, 64 * (q + 1))
            nc.vector.tensor_tensor(
                z_g[:, places, :].rearrange("p (c i) t -> p c t i", i=4),
                st[:, :, places].rearrange("p t (c i) -> p c t i", i=4),
                g2[q][:].rearrange("p t (c i) -> p c t i", i=4),
                ALU.subtract,
            )

        def make_a(h):
            places = slice(128 * h, 128 * (h + 1))
            nc.vector.quantize_mx(
                out=z_codes[:, places].bitcast(FP8X4),
                scales=z_scales[:, places],
                in_=z_g[:, places, :].rearrange("p c t -> p (c t)"),
            )
            for t in range(PACK):
                product(a_ps[h][t // 2][:, t % 2, :], w2_q, t, (z_codes, z_scales), places)

        def take_a(h, q):
            pair = win_c[2 * q][:].rearrange("p (e c) -> p e c", e=2)
            nc.vector.tensor_copy(pair[:, :, 128 * h : 128 * (h + 1)], a_ps[h][q][:])

        take_b(0)
        make_z(0)
        take_b(1)
        make_z(1)
        make_bias(0)
        take_b(2)
        make_a(0)
        make_z(2)
        take_a(0, 0)
        make_z(3)
        take_b(3)
        make_a(1)
        make_bias(1)
        take_a(0, 1)
        take_a(1, 0)
        take_a(1, 1)

        ea = sb.tile([P, PACK, S], F32, name="ea")
        for t in range(PACK):
            nc.scalar.activation(
                ea[:, t, :], win[t][:].indirect(n4_t[:]), ACT.Exp, bias=bias[:, t : t + 1], scale=tau_t[:, t : t + 1]
            )
        quad = sb.tile([P, 2, S], F32, name="quad")
        for t in range(2):
            nc.vector.scalar_tensor_tensor(quad[:, t, :], ea[:, t, :], 0.5, ea[:, t, :], ALU.add, ALU.mult)
        nc.scalar.activation(win[3][:], quad[:].rearrange("p e c -> p (e c)"), ACT.Abs_reciprocal_sqrt, bias=0.25, scale=4.0)
        nc.scalar.activation(
            win[2][:], ea[:, 2:, :].rearrange("p e c -> p (e c)"), ACT.Abs_reciprocal_sqrt, bias=0.5, scale=2.0
        )
        inverse = [win[3][:, :S], win[3][:, S:]]
        for t in range(2):
            square = sb.tile([P, S], F32, name="square%d" % t)
            nc.scalar.activation(square[:], win[2][:, t * S : (t + 1) * S], ACT.Square)
            inverse.append(square[:])

        diff = [sb.tile([P, S], F32, name="diff%d" % t) for t in range(PACK)]
        for q in range(2):
            even, odd = win_c[2 * q], win_c[2 * q + 1]
            nc.vector.tensor_copy(odd[:, S:], even[:, :S])
            nc.vector.tensor_copy(odd[:, :S], even[:, S:])
            nc.vector.tensor_tensor(diff[2 * q][:], even[:].indirect(n5_t[:]), odd[:, S:], ALU.subtract)
            nc.vector.tensor_tensor(diff[2 * q + 1][:], odd[:].indirect(n5_t[:]), even[:, S:], ALU.subtract)

        out_rows = out.rearrange("(t p) c -> p t c", p=P)
        res = [sb.tile([P, S], F32, name="res%d" % t) for t in range(PACK)]
        for t in range(PACK):
            nc.vector.scalar_tensor_tensor(res[t][:], diff[t][:], -1.0, inverse[t], ALU.mult, ALU.mult)
            nc.sync.dma_start(out=out_rows[:, t, :], in_=res[t][:])
